import numpy as np
import ml_dtypes


def mxq(x, axis, fmt="e4m3"):
    dtype, down = {"e4m3": (ml_dtypes.float8_e4m3fn, 7), "e5m2": (ml_dtypes.float8_e5m2, 14)}[fmt]
    v = np.moveaxis(np.asarray(x, np.float32).astype(ml_dtypes.bfloat16).astype(np.float64), axis, -1)
    blocks = v.reshape(v.shape[:-1] + (-1, 32))
    amax = np.abs(blocks).max(-1, keepdims=True)
    byte = np.maximum(np.where(amax > 0, np.frexp(amax)[1] - 1 + 127, 0) - down, 1)
    scale = np.exp2(byte - 127.0)
    codes = (blocks / scale).astype(np.float32).astype(dtype).astype(np.float64)
    return np.moveaxis((codes * scale).reshape(v.shape), -1, axis)


WIDE = False


def mx_kscale(k):
    if not WIDE:
        return np.ones(k)
    levels = np.array([10, -10, 5, -5, 0])
    if k % 512:
        return np.exp2(np.random.permutation(np.resize(levels, k // 32))).repeat(32)
    a = np.empty((k // 512, 16))
    for p in range(k // 512):
        a[p, :8] = np.random.permutation(np.resize(levels, 8))
        for g in range(8):
            far = levels[np.abs(levels - a[p, g]) >= 10]
            a[p, g + 8] = far[np.random.randint(len(far))]
    return np.exp2(a.ravel()).repeat(32)


def f64(x):
    return np.asarray(x).astype(np.float64)


def striped(idx):
    return np.tile(idx.reshape(-1, 16).T, (8, 1)).astype(np.uint16)


def unstriped(offs):
    return offs[:16].T.reshape(-1).astype(np.int64)


def striped8(idx):
    return np.concatenate([x.reshape(-1, 16).T for x in idx]).astype(np.uint16)


def runs(offs, k):
    lists = np.stack([offs[16 * r : 16 * r + 16].T.reshape(-1) for r in range(8)]).astype(np.int64)
    return lists[np.arange(k) % 512 // 64]


def pack_weight(w):
    k, n = w.shape
    w = f64(np.asarray(w, np.float32).astype(ml_dtypes.bfloat16)).reshape(k // 32, 32, n)
    amax = np.abs(w).max(1)
    byte = np.clip(np.where(amax > 0, np.frexp(amax)[1] - 1 + 127 - 7, 1), 1, 254)
    scaled = (w * np.exp2(127.0 - byte)[:, None, :]).reshape(k, n).astype(np.float32)
    words = np.ascontiguousarray(scaled.reshape(k // 512, 128, 4, n).transpose(0, 1, 3, 2)).astype(ml_dtypes.float8_e4m3fn).view(np.uint8)
    return words, np.ascontiguousarray(byte.astype(np.uint8).reshape(k // 512, 16, n))


def unpack_weight(words, scales):
    g, p, n, _ = words.shape
    vals = np.ascontiguousarray(words).view(ml_dtypes.float8_e4m3fn).astype(np.float64) * np.repeat(np.exp2(scales.astype(np.float64) - 127.0), 8, axis=1)[..., None]
    return vals.transpose(0, 1, 3, 2).reshape(g * 512, n)


E2M1 = np.array([0.0, 0.5, 1.0, 1.5, 2.0, 3.0, 4.0, 6.0, -0.0, -0.5, -1.0, -1.5, -2.0, -3.0, -4.0, -6.0])


def pack_fp4(w):
    k, n = w.shape
    w = f64(np.asarray(w, np.float32).astype(ml_dtypes.bfloat16)).reshape(k // 32, 32, n)
    amax = np.abs(w).max(1)
    mant, ex = np.frexp(amax / 6.0)
    byte = np.clip(np.where(amax > 0, np.where(mant > 0.5, ex, ex - 1) + 127, 1), 1, 254)
    scaled = (w * np.exp2(127.0 - byte)[:, None, :]).reshape(k, n).astype(np.float32)
    c = np.ascontiguousarray(scaled.reshape(k // 512, 128, 4, n).transpose(0, 1, 3, 2)).astype(ml_dtypes.float4_e2m1fn).view(np.uint8) & 0xF
    words = (c[..., 0::2] | (c[..., 1::2] << 4)).reshape(k // 512, 128, 2 * n)
    return np.ascontiguousarray(words), np.ascontiguousarray(byte.astype(np.uint8).reshape(k // 512, 16, n))


def unpack_fp4(words, scales):
    g, _, n = scales.shape
    words = np.ascontiguousarray(words).reshape(g, 128, n, 2)
    nib = np.empty((g, 128, n, 4), np.uint8)
    nib[..., 0::2] = words & 0xF
    nib[..., 1::2] = words >> 4
    vals = E2M1[nib] * np.repeat(np.exp2(scales.astype(np.float64) - 127.0), 8, axis=1)[..., None]
    return vals.transpose(0, 1, 3, 2).reshape(g * 512, n)


def planes(y):
    n, m = y.shape
    v = y.astype(np.float32).astype(ml_dtypes.bfloat16).astype(np.float64).reshape(n // 32, 32, m)
    top = np.abs(v).max(1)
    byte = np.clip(np.where(top > 0, np.frexp(top)[1] - 1 + 127 - 7, 1), 1, 254)
    codes = (v * np.exp2(127.0 - byte)[:, None, :]).reshape(n, m).astype(np.float32).astype(ml_dtypes.float8_e4m3fn).view(np.uint8)
    words = codes.reshape(n // 512, 128, 4, m).transpose(0, 1, 3, 2)
    return np.ascontiguousarray(words), np.ascontiguousarray(byte.astype(np.uint8).reshape(n // 512, 16, m))


K, T, S, H, G = 512, 1024, 512, 512, 2048


def setup_inputs():
    n = np.random.standard_normal
    s = mx_kscale(K)[:, None]
    packed_xT = pack_weight(n((K, T)) * s)
    packed_w1 = pack_fp4(n((K, H)) / np.sqrt(K) / s)
    packed_w2 = pack_fp4(n((K, H)) / np.sqrt(K) / s)
    packed_dT = pack_weight(n((K, G)) / s)
    return {
        "x_words": packed_xT[0],
        "x_scales": packed_xT[1],
        "w1_words": packed_w1[0],
        "w1_scales": packed_w1[1],
        "w2_words": packed_w2[0],
        "w2_scales": packed_w2[1],
        "tau": np.random.uniform(0.3, 0.9, (H, 1)).astype(np.float32),
        "gs": (np.random.uniform(0.5, 1.5, (K, 1)) * s).astype(np.float32),
        "d_words": packed_dT[0],
        "d_scales": packed_dT[1],
        "tau2": np.random.uniform(0.3, 0.9, (H, 1)).astype(np.float32),
        "offs": striped(np.random.permutation(T)[:S]),
        "two": striped(np.random.permutation(T)[:S]),
        "n1": striped8(np.stack([np.random.permutation(S) for _ in range(8)])),
        "n2": striped8(np.stack([np.random.permutation(S) for _ in range(8)])),
        "k1": striped8(np.random.randint(0, G, (8, H))),
        "n3": striped(np.random.permutation(S)),
    }


def reference(x_words, x_scales, w1_words, w1_scales, w2_words, w2_scales, tau, gs, d_words, d_scales, tau2, offs, two, n1, n2, k1, n3):
    d_k1 = unpack_weight(d_words, d_scales)[np.arange(K)[:, None], runs(k1, K)]
    x_two = unpack_weight(x_words, x_scales)[:, unstriped(two)]
    d = unpack_fp4(w2_words, w2_scales).T @ x_two
    top = d.max(axis=1, keepdims=True)
    ea = np.exp(f64(tau) * (d[np.arange(H)[:, None], runs(n1, H)] - top))
    xq = unpack_weight(x_words, x_scales)[:, unstriped(offs)]
    y = unpack_fp4(w1_words, w1_scales).T @ xq
    z = f64(gs) * ((2.0 * ea) * (y - (y[np.arange(H)[:, None], runs(n2, H)])) - (0.5 * d))
    h = 0.0625 * ((d_k1.T @ mxq(z, 0, "e4m3")))
    top2 = h.max(axis=1, keepdims=True)
    own = np.exp(f64(tau2) * (h - top2))
    ea2 = np.exp(f64(tau2) * (h[:, unstriped(n3)] - top2))
    out_0 = (2.0 * (h * own)) / (own + ea2 + 0.25)
    return (out_0,) + planes(out_0)

@@ -1,0 +1,294 @@
+from contextlib import ExitStack
+
+import concourse.mybir as mybir
+
+K, T, S, H, G = 512, 1024, 512, 512, 2048
+FLOPS = 3 * 2 * K * H * S
+
+F32 = mybir.dt.float32
+BF16 = mybir.dt.bfloat16
+I32 = mybir.dt.int32
+U32 = mybir.dt.uint32
+U16 = mybir.dt.uint16
+U8 = mybir.dt.uint8
+FP8X4 = mybir.dt.float8_e4m3fn_x4
+FP4X4 = mybir.dt.float4_e2m1fn_x4
+ALU = mybir.AluOpType
+ACT = mybir.ActivationFunctionType
+
+P = 128
+PACK = 4
+HALF = S // 2
+PIECES = (256, 256)
+CHUNKS = (128, 128, 128, 128)
+
+
+def spans(widths):
+    return [slice(sum(widths[:i]), sum(widths[: i + 1])) for i in range(len(widths))]
+
+
+def tile_picked_twqpxbesh_none_po_kernel(
+    tc, x_words, x_scales, w1_words, w1_scales, w2_words, w2_scales, tau, gs, d_words, d_scales, tau2,
+    offs, two, n1, n2, k1, n3, out_0, out_1, out_2,
+):
+    nc = tc.nc
+    with ExitStack() as ctx:
+        sb = ctx.enter_context(tc.tile_pool(name="sb", bufs=1))
+        ps = ctx.enter_context(tc.psum_pool(name="ps", bufs=1))
+
+        def tile(name, shape, dtype, tag=""):
+            return sb.tile(shape, dtype, name=name, tag=tag or name, align_bytes=64)
+
+        def load_list(name, src):
+            dst = sb.tile([P, S // 16], U16, name=name)
+            nc.sync.dma_start(dst[:], src)
+            return dst
+
+        def zero(engine, dst):
+            engine.memset(dst[:].bitcast(I32), 0)
+
+        def load_scale_rows(queue, dst, src, q):
+            queue.dma_start(dst[32 * q : 32 * q + 4, :].bitcast(I32), src[0, 4 * q : 4 * q + 4, :].bitcast(I32))
+
+        def load_rows(queue, name, src):
+            dst = tile(name, [P, PACK], F32)
+            queue.dma_start(dst[:], src.rearrange("(p t) o -> p (t o)", t=PACK))
+            return dst
+
+        def deal(engine_copy, dst, src):
+            engine_copy(dst.rearrange("p (t m) -> p t m", t=PACK), src.rearrange("p (m t) -> p t m", t=PACK))
+
+        def entries(lst, c):
+            return lst[:, c.start // 16 : c.stop // 16]
+
+        xs = tile("xs", [P, T], U8)
+        w2s_raw = tile("w2s_raw", [P, H], U8)
+        w1s_raw = tile("w1s_raw", [P, H], U8)
+        ds = tile("ds", [P, G], U8)
+        dk_scales = tile("dk_scales", [P, H], U8)
+        zero(nc.gpsimd, xs)
+        zero(nc.gpsimd, w2s_raw)
+        zero(nc.vector, w1s_raw)
+        zero(nc.vector, ds)
+        zero(nc.vector, dk_scales)
+
+        xw = tile("xw", [P, T], U32, tag="window")
+        w2w_raw = tile("w2w_raw", [P, 2 * H], U8)
+        w1w_raw = tile("w1w_raw", [P, 2 * H], U8)
+        dw = tile("dw", [P, G], U32)
+        two_l = load_list("two_l", two)
+        load_scale_rows(nc.sync, xs, x_scales, 0)
+        load_scale_rows(nc.scalar, xs, x_scales, 1)
+        load_scale_rows(nc.scalar, xs, x_scales, 2)
+        load_scale_rows(nc.scalar, xs, x_scales, 3)
+        nc.sync.dma_start(w2w_raw[:].bitcast(I32), w2_words[0].bitcast(I32))
+        nc.sync.dma_start(xw[:].bitcast(I32), x_words[0].rearrange("p n t -> p (n t)").bitcast(I32))
+        load_scale_rows(nc.scalar, w2s_raw, w2_scales, 0)
+        load_scale_rows(nc.scalar, w2s_raw, w2_scales, 1)
+        load_scale_rows(nc.sync, w2s_raw, w2_scales, 2)
+        load_scale_rows(nc.sync, w2s_raw, w2_scales, 3)
+        offs_l = load_list("offs_l", offs)
+        nc.sync.dma_start(w1w_raw[:].bitcast(I32), w1_words[0].bitcast(I32))
+        tau_t = load_rows(nc.sync, "tau_t", tau)
+        n1_l = load_list("n1_l", n1)
+        n2_l = load_list("n2_l", n2)
+        k1_l = load_list("k1_l", k1)
+        nc.sync.dma_start(dw[:].bitcast(I32), d_words[0].rearrange("p n t -> p (n t)").bitcast(I32))
+        load_scale_rows(nc.gpsimd, w1s_raw, w1_scales, 0)
+        load_scale_rows(nc.gpsimd, w1s_raw, w1_scales, 1)
+        load_scale_rows(nc.gpsimd, w1s_raw, w1_scales, 2)
+        load_scale_rows(nc.gpsimd, w1s_raw, w1_scales, 3)
+        gs_t = load_rows(nc.gpsimd, "gs_t", gs)
+        nc.gpsimd.dma_start(ds[0:P:8, :].bitcast(I32), d_scales[0].bitcast(I32))
+        tau2_t = load_rows(nc.sync, "tau2_t", tau2)
+        n3_l = load_list("n3_l", n3)
+
+        w2w = tile("w2w", [P, 2 * H], U8)
+        w2s = tile("w2s", [P, H], U8)
+        w1w = tile("w1w", [P, 2 * H], U8, tag="late_ea2")
+        w1s = tile("w1s", [P, H], U8, tag="late_ea3")
+        deal(nc.scalar.copy, w2w[:].bitcast(U16), w2w_raw[:].bitcast(U16))
+        ntau = tile("ntau", [P, PACK], F32)
+        nc.scalar.activation(ntau[:], tau_t[:], ACT.Copy, scale=-1.0)
+        deal(nc.scalar.copy, w1w[:].bitcast(U16), w1w_raw[:].bitcast(U16))
+        deal(nc.gpsimd.tensor_copy, w1s[:], w1s_raw[:])
+        gs2 = tile("gs2", [P, PACK], F32)
+        nc.gpsimd.tensor_scalar(gs2[:], gs_t[:], 2.0, 0.0, op0=ALU.mult, op1=ALU.add)
+        gsh = tile("gsh", [P, PACK], F32)
+        nc.gpsimd.tensor_scalar(gsh[:], gs_t[:], -0.5, 0.0, op0=ALU.mult, op1=ALU.add)
+        ntau2 = tile("ntau2", [P, PACK], F32)
+        nc.gpsimd.tensor_scalar(ntau2[:], tau2_t[:], -1.0, 0.0, op0=ALU.mult, op1=ALU.add)
+
+        x2s = tile("x2s", [P, S], U8)
+        x2w = tile("x2w", [P, S], U32, tag="picked_words")
+        x1s = tile("x1s", [P, S], U8)
+        nc.vector.tensor_copy(x2s[:], xs[:].indirect(two_l[:]))
+        nc.vector.tensor_copy(x2w[:], xw[:].indirect(two_l[:]))
+        deal(nc.vector.tensor_copy, w2s[:], w2s_raw[:])
+
+        def project(bank, words, scales, xwords, xscales, t):
+            nc.tensor.matmul_mx(
+                bank[:],
+                lhsT=words[:, 2 * P * t : 2 * P * (t + 1)].bitcast(FP4X4),
+                lhsT_scale=scales[:, P * t : P * (t + 1)],
+                rhs=xwords[:].bitcast(FP8X4),
+                rhs_scale=xscales[:],
+                start=True,
+                stop=True,
+            )
+
+        d_ps = [ps.tile([P, S], F32, name=f"d_ps{t}", tag=f"a{t}") for t in range(PACK)]
+        y_ps = [ps.tile([P, S], F32, name=f"y_ps{t}", tag=f"b{t}") for t in range(PACK)]
+        for t in range(PACK):
+            project(d_ps[t], w2w, w2s, x2w, x2s, t)
+
+        d = [tile(f"d{t}", [P, S], F32) for t in range(PACK)]
+        y = [tile(f"y{t}", [P, S], F32) for t in range(PACK)]
+        top = tile("top", [P, PACK], F32)
+        bias = tile("bias", [P, PACK], F32)
+        yg = tile("yg", [P, PACK, S], F32)
+
+        def leave_with_max(dst, bank, factor, largest):
+            nc.vector.tensor_scalar(dst[:], bank[:], factor, None, op0=ALU.mult, op1=ALU.max, accum_out=largest)
+
+        def fetch_exp(dst, window, offsets, scale, shift):
+            nc.scalar.activation(dst, window[:].indirect(offsets), ACT.Exp, bias=shift, scale=scale)
+
+        nc.vector.tensor_copy(x1s[:], xs[:].indirect(offs_l[:]))
+        leave_with_max(d[0], d_ps[0], 1.0, top[:, 0:1])
+        leave_with_max(d[1], d_ps[1], 1.0, top[:, 1:2])
+        x1w = tile("x1w", [P, S], U32, tag="picked_words")
+        nc.vector.tensor_copy(x1w[:], xw[:].indirect(offs_l[:]))
+        leave_with_max(d[2], d_ps[2], 1.0, top[:, 2:3])
+        leave_with_max(d[3], d_ps[3], 1.0, top[:, 3:4])
+        for t in range(PACK):
+            project(y_ps[t], w1w, w1s, x1w, x1s, t)
+
+        halves = spans((HALF, HALF))
+        HOLD = (2, 3)
+        ea = [[tile(f"ea{t}_{i}", [P, HALF], F32, tag=f"late_ea{t}" if i == 1 and t in HOLD else "") for i in range(2)] for t in range(PACK)]
+
+        def fetch_ea(t, i):
+            fetch_exp(ea[t][i][:], d[t], entries(n1_l, halves[i]), tau_t[:, t : t + 1], bias[:, t : t + 1])
+
+        for t in range(PACK):
+            nc.scalar.activation(bias[:, t : t + 1], top[:, t : t + 1], ACT.Copy, scale=ntau[:, t : t + 1])
+            fetch_ea(t, 0)
+            if t not in HOLD:
+                fetch_ea(t, 1)
+
+        dk_raw = tile("dk_raw", [P, H], U32, tag="picked_words")
+        dk = tile("dk", [P, H], U32)
+        dks_raw = tile("dks_raw", [P, H], U8, tag="window")
+        dks_dealt = tile("dks_dealt", [P, H], U8)
+        nc.vector.tensor_copy(dks_raw[:], ds[:].indirect(k1_l[:]))
+        nc.vector.tensor_copy(dk_raw[:], dw[:].indirect(k1_l[:]))
+        deal(nc.vector.tensor_copy, dks_dealt[:], dks_raw[:])
+        deal(nc.vector.tensor_copy, dk[:], dk_raw[:])
+        for q in range(4):
+            nc.sync.dma_start(
+                dk_scales[32 * q : 32 * q + 4, :].bitcast(I32), dks_dealt[32 * q : 32 * q + 32 : 8, :].bitcast(I32)
+            )
+
+        diff = tile("diff", [P, PACK, S], F32)
+        gated = tile("gated", [P, PACK, S], F32)
+        zb = tile("zb", [P, PACK, S], BF16)
+        z_codes = tile("z_codes", [P, S], U32)
+        z_scales = tile("z_scales", [P, S], U8)
+
+        def interleave(engine_copy, dst, src):
+            engine_copy(dst.rearrange("p (c i t) -> p c t i", i=4, t=PACK), src.rearrange("p t (c i) -> p c t i", i=4))
+
+        pieces = spans(PIECES)
+        for i, c in enumerate(pieces):
+            half = c.start // HALF
+            ch = slice(c.start - half * HALF, c.stop - half * HALF)
+            for t in range(PACK):
+                if i == 0:
+                    if t in ():
+                        nc.vector.tensor_scalar(y[t][:], y_ps[t][:], gs2[:, t : t + 1], None, op0=ALU.mult)
+                    else:
+                        nc.scalar.activation(y[t][:], y_ps[t][:], ACT.Copy, scale=gs2[:, t : t + 1])
+                if c.start == HALF and t in HOLD:
+                    fetch_ea(t, 1)
+                nc.scalar.activation(yg[:, t, c], y[t][:].indirect(entries(n2_l, c)), ACT.Copy)
+            for step in range(PACK + 2):
+                if step < PACK:
+                    nc.vector.scalar_tensor_tensor(
+                        diff[:, step, c], y_ps[step][:, c], gs2[:, step : step + 1], yg[:, step, c],
+                        op0=ALU.mult, op1=ALU.subtract,
+                    )
+                if 0 <= step - 1 < PACK:
+                    t = step - 1
+                    eng = nc.gpsimd if False else nc.vector
+                    eng.tensor_tensor(gated[:, t, c], diff[:, t, c], ea[t][half][:, ch], ALU.mult)
+                if 0 <= step - 2 < PACK:
+                    t = step - 2
+                    nc.vector.scalar_tensor_tensor(
+                        zb[:, t, c], d_ps[t][:, c], gsh[:, t : t + 1], gated[:, t, c], op0=ALU.mult, op1=ALU.add
+                    )
+            z4 = tile(f"z4_{i}", [P, PIECES[i] * PACK], BF16)
+            interleave(nc.scalar.copy if i in () else nc.vector.tensor_copy, z4[:], zb[:, :, c])
+            nc.vector.quantize_mx(z_codes[:, c].bitcast(FP8X4), z_scales[:, c], z4[:])
+        h_ps = [ps.tile([P, S], F32, name=f"h_ps{t}", tag=f"b{t}") for t in range(PACK)]
+        for c in pieces:
+            for t in range(PACK):
+                nc.tensor.matmul_mx(
+                    h_ps[t][:, c],
+                    lhsT=dk[:, P * t : P * (t + 1)].bitcast(FP8X4),
+                    lhsT_scale=dk_scales[:, P * t : P * (t + 1)],
+                    rhs=z_codes[:, c].bitcast(FP8X4),
+                    rhs_scale=z_scales[:, c],
+                    start=True,
+                    stop=True,
+                )
+
+        h = [tile(f"h{t}", [P, S], F32) for t in range(PACK)]
+        top2 = tile("top2", [P, PACK], F32)
+        bias2 = [tile(f"bias2_{t}", [P, 1], F32) for t in range(PACK)]
+        own = tile("own", [P, PACK, S], F32)
+        ea2 = tile("ea2", [P, PACK, S], F32)
+        den = tile("den", [P, PACK, S], F32)
+        num = tile("num", [P, PACK, S], F32)
+        den_sq = tile("den_sq", [P, PACK, S], F32)
+        for t in range(PACK):
+            leave_with_max(h[t], h_ps[t], 0.0625, top2[:, t : t + 1])
+            if t == 0:
+                nc.scalar.activation(bias2[t][:], top2[:, t : t + 1], ACT.Copy, scale=ntau2[:, t : t + 1])
+            else:
+                nc.vector.tensor_tensor(bias2[t][:], top2[:, t : t + 1], ntau2[:, t : t + 1], ALU.mult)
+        for t in range(PACK):
+            nc.scalar.activation(own[:, t, :], h[t][:], ACT.Exp, bias=bias2[t][:], scale=tau2_t[:, t : t + 1])
+            for c in halves:
+                fetch_exp(ea2[:, t, c], h[t], entries(n3_l, c), tau2_t[:, t : t + 1], bias2[t][:])
+            nc.vector.scalar_tensor_tensor(num[:, t, :], h_ps[t][:], 0.125, own[:, t, :], op0=ALU.mult, op1=ALU.mult)
+            for c in halves:
+                nc.vector.scalar_tensor_tensor(den[:, t, c], own[:, t, c], 0.25, ea2[:, t, c], op0=ALU.add, op1=ALU.add)
+            for c in halves:
+                nc.vector.tensor_tensor(den_sq[:, t, c], den[:, t, c], den[:, t, c], ALU.mult)
+
+        inv = tile("inv", [P, PACK, S], F32)
+        res = tile("res", [P, PACK, S], F32)
+        o_codes = tile("o_codes", [P, S], U32)
+        o_scales = tile("o_scales", [P, S], U8)
+        out_rows = out_0.rearrange("(p t) c -> p t c", t=PACK)
+        out_words = out_1[0].rearrange("p n t -> p (n t)").bitcast(I32)
+        chunks = spans(CHUNKS)
+        o4 = [tile(f"o4_{i}", [P, CHUNKS[i] * PACK], BF16) for i in range(len(chunks))]
+        for c in chunks:
+            nc.scalar.activation(inv[:, :, c], den_sq[:, :, c], ACT.Abs_reciprocal_sqrt)
+        for step in range(len(chunks) + 2):
+            if step < len(chunks):
+                c = chunks[step]
+                nc.vector.tensor_tensor(res[:, :, c], num[:, :, c], inv[:, :, c], ALU.mult)
+                nc.sync.dma_start(out_rows[:, :, c], res[:, :, c])
+            if 0 <= step - 1 < len(chunks):
+                copy = nc.scalar.copy if step - 1 in (0, 1) else nc.vector.tensor_copy
+                interleave(copy, o4[step - 1][:], res[:, :, chunks[step - 1]])
+            if 0 <= step - 2 < len(chunks):
+                c = chunks[step - 2]
+                nc.vector.quantize_mx(o_codes[:, c].bitcast(FP8X4), o_scales[:, c], o4[step - 2][:])
+                nc.sync.dma_start(out_words[:, c], o_codes[:, c].bitcast(I32))
+        for q in range(4):
+            queue = nc.scalar if q % 2 else nc.sync
+            queue.dma_start(out_2[0, 4 * q : 4 * q + 4, :].bitcast(I32), o_scales[32 * q : 32 * q + 4, :].bitcast(I32))

@@ -67,8 +67,8 @@ def tile_picked_twqpxbesh_none_po_kernel(
         ds = tile("ds", [P, G], U8)
         dk_scales = tile("dk_scales", [P, H], U8)
         zero(nc.gpsimd, xs)
-        zero(nc.gpsimd, w2s_raw)
-        zero(nc.vector, w1s_raw)
+        zero(nc.gpsimd, w1s_raw)
+        zero(nc.vector, w2s_raw)
         zero(nc.vector, ds)
         zero(nc.vector, dk_scales)
 
@@ -76,55 +76,58 @@ def tile_picked_twqpxbesh_none_po_kernel(
         w2w_raw = tile("w2w_raw", [P, 2 * H], U8)
         w1w_raw = tile("w1w_raw", [P, 2 * H], U8)
         dw = tile("dw", [P, G], U32)
-        two_l = load_list("two_l", two)
+        offs_l = load_list("offs_l", offs)
         load_scale_rows(nc.sync, xs, x_scales, 0)
         load_scale_rows(nc.scalar, xs, x_scales, 1)
         load_scale_rows(nc.scalar, xs, x_scales, 2)
         load_scale_rows(nc.scalar, xs, x_scales, 3)
-        nc.sync.dma_start(w2w_raw[:].bitcast(I32), w2_words[0].bitcast(I32))
+        nc.sync.dma_start(w1w_raw[:].bitcast(I32), w1_words[0].bitcast(I32))
+        load_scale_rows(nc.sync, w1s_raw, w1_scales, 0)
         nc.sync.dma_start(xw[:].bitcast(I32), x_words[0].rearrange("p n t -> p (n t)").bitcast(I32))
-        load_scale_rows(nc.scalar, w2s_raw, w2_scales, 0)
-        load_scale_rows(nc.scalar, w2s_raw, w2_scales, 1)
+        load_scale_rows(nc.sync, w1s_raw, w1_scales, 1)
+        load_scale_rows(nc.sync, w1s_raw, w1_scales, 2)
+        load_scale_rows(nc.sync, w1s_raw, w1_scales, 3)
+        two_l = load_list("two_l", two)
+        nc.sync.dma_start(w2w_raw[:].bitcast(I32), w2_words[0].bitcast(I32))
+        gs_t = load_rows(nc.sync, "gs_t", gs)
+        load_scale_rows(nc.sync, w2s_raw, w2_scales, 0)
+        load_scale_rows(nc.sync, w2s_raw, w2_scales, 1)
         load_scale_rows(nc.sync, w2s_raw, w2_scales, 2)
         load_scale_rows(nc.sync, w2s_raw, w2_scales, 3)
-        offs_l = load_list("offs_l", offs)
-        nc.sync.dma_start(w1w_raw[:].bitcast(I32), w1_words[0].bitcast(I32))
-        tau_t = load_rows(nc.sync, "tau_t", tau)
-        n1_l = load_list("n1_l", n1)
-        n2_l = load_list("n2_l", n2)
         k1_l = load_list("k1_l", k1)
+        nc.sync.dma_start(ds[0:P:8, :].bitcast(I32), d_scales[0].bitcast(I32))
+        tau_t = load_rows(nc.sync, "tau_t", tau)
+        n2_l = load_list("n2_l", n2)
+        n1_l = load_list("n1_l", n1)
         nc.sync.dma_start(dw[:].bitcast(I32), d_words[0].rearrange("p n t -> p (n t)").bitcast(I32))
-        load_scale_rows(nc.gpsimd, w1s_raw, w1_scales, 0)
-        load_scale_rows(nc.gpsimd, w1s_raw, w1_scales, 1)
-        load_scale_rows(nc.gpsimd, w1s_raw, w1_scales, 2)
-        load_scale_rows(nc.gpsimd, w1s_raw, w1_scales, 3)
-        gs_t = load_rows(nc.gpsimd, "gs_t", gs)
-        nc.gpsimd.dma_start(ds[0:P:8, :].bitcast(I32), d_scales[0].bitcast(I32))
         tau2_t = load_rows(nc.sync, "tau2_t", tau2)
         n3_l = load_list("n3_l", n3)
 
         w2w = tile("w2w", [P, 2 * H], U8)
         w2s = tile("w2s", [P, H], U8)
-        w1w = tile("w1w", [P, 2 * H], U8, tag="late_ea2")
-        w1s = tile("w1s", [P, H], U8, tag="late_ea3")
-        deal(nc.scalar.copy, w2w[:].bitcast(U16), w2w_raw[:].bitcast(U16))
-        ntau = tile("ntau", [P, PACK], F32)
-        nc.scalar.activation(ntau[:], tau_t[:], ACT.Copy, scale=-1.0)
-        deal(nc.scalar.copy, w1w[:].bitcast(U16), w1w_raw[:].bitcast(U16))
-        deal(nc.gpsimd.tensor_copy, w1s[:], w1s_raw[:])
+        w1w = tile("w1w", [P, 2 * H], U8)
+        w1s = tile("w1s", [P, H], U8)
         gs2 = tile("gs2", [P, PACK], F32)
-        nc.gpsimd.tensor_scalar(gs2[:], gs_t[:], 2.0, 0.0, op0=ALU.mult, op1=ALU.add)
         gsh = tile("gsh", [P, PACK], F32)
-        nc.gpsimd.tensor_scalar(gsh[:], gs_t[:], -0.5, 0.0, op0=ALU.mult, op1=ALU.add)
+        ntau = tile("ntau", [P, PACK], F32)
         ntau2 = tile("ntau2", [P, PACK], F32)
+        deal(nc.scalar.copy, w1w[:].bitcast(U16), w1w_raw[:].bitcast(U16))
+        nc.scalar.activation(gs2[:], gs_t[:], ACT.Copy, scale=2.0)
+        deal(nc.scalar.copy, w2w[:].bitcast(U16), w2w_raw[:].bitcast(U16))
+        deal(nc.gpsimd.tensor_copy, w2s[:], w2s_raw[:])
+        nc.gpsimd.tensor_scalar(gsh[:], gs_t[:], -0.5, 0.0, op0=ALU.mult, op1=ALU.add)
+        nc.gpsimd.tensor_scalar(ntau[:], tau_t[:], -1.0, 0.0, op0=ALU.mult, op1=ALU.add)
         nc.gpsimd.tensor_scalar(ntau2[:], tau2_t[:], -1.0, 0.0, op0=ALU.mult, op1=ALU.add)
 
-        x2s = tile("x2s", [P, S], U8)
-        x2w = tile("x2w", [P, S], U32, tag="picked_words")
         x1s = tile("x1s", [P, S], U8)
+        x1w = tile("x1w", [P, S], U32)
+        x2s = tile("x2s", [P, S], U8)
+        x2w = tile("x2w", [P, S], U32)
+        nc.vector.tensor_copy(x1s[:], xs[:].indirect(offs_l[:]))
+        nc.vector.tensor_copy(x1w[:], xw[:].indirect(offs_l[:]))
+        deal(nc.vector.tensor_copy, w1s[:], w1s_raw[:])
         nc.vector.tensor_copy(x2s[:], xs[:].indirect(two_l[:]))
         nc.vector.tensor_copy(x2w[:], xw[:].indirect(two_l[:]))
-        deal(nc.vector.tensor_copy, w2s[:], w2s_raw[:])
 
         def project(bank, words, scales, xwords, xscales, t):
             nc.tensor.matmul_mx(
@@ -140,13 +143,18 @@ def tile_picked_twqpxbesh_none_po_kernel(
         d_ps = [ps.tile([P, S], F32, name=f"d_ps{t}", tag=f"a{t}") for t in range(PACK)]
         y_ps = [ps.tile([P, S], F32, name=f"y_ps{t}", tag=f"b{t}") for t in range(PACK)]
         for t in range(PACK):
+            project(y_ps[t], w1w, w1s, x1w, x1s, t)
+        for t in range(PACK):
             project(d_ps[t], w2w, w2s, x2w, x2s, t)
 
         d = [tile(f"d{t}", [P, S], F32) for t in range(PACK)]
         y = [tile(f"y{t}", [P, S], F32) for t in range(PACK)]
         top = tile("top", [P, PACK], F32)
-        bias = tile("bias", [P, PACK], F32)
+        bias = [tile(f"bias_{t}", [P, 1], F32) for t in range(PACK)]
         yg = tile("yg", [P, PACK, S], F32)
+        ea = tile("ea", [P, PACK, S], F32)
+        halves = spans((HALF, HALF))
+        pieces = spans(PIECES)
 
         def leave_with_max(dst, bank, factor, largest):
             nc.vector.tensor_scalar(dst[:], bank[:], factor, None, op0=ALU.mult, op1=ALU.max, accum_out=largest)
@@ -154,36 +162,27 @@ def tile_picked_twqpxbesh_none_po_kernel(
         def fetch_exp(dst, window, offsets, scale, shift):
             nc.scalar.activation(dst, window[:].indirect(offsets), ACT.Exp, bias=shift, scale=scale)
 
-        nc.vector.tensor_copy(x1s[:], xs[:].indirect(offs_l[:]))
-        leave_with_max(d[0], d_ps[0], 1.0, top[:, 0:1])
-        leave_with_max(d[1], d_ps[1], 1.0, top[:, 1:2])
-        x1w = tile("x1w", [P, S], U32, tag="picked_words")
-        nc.vector.tensor_copy(x1w[:], xw[:].indirect(offs_l[:]))
-        leave_with_max(d[2], d_ps[2], 1.0, top[:, 2:3])
-        leave_with_max(d[3], d_ps[3], 1.0, top[:, 3:4])
-        for t in range(PACK):
-            project(y_ps[t], w1w, w1s, x1w, x1s, t)
-
-        halves = spans((HALF, HALF))
-        HOLD = (2, 3)
-        ea = [[tile(f"ea{t}_{i}", [P, HALF], F32, tag=f"late_ea{t}" if i == 1 and t in HOLD else "") for i in range(2)] for t in range(PACK)]
-
-        def fetch_ea(t, i):
-            fetch_exp(ea[t][i][:], d[t], entries(n1_l, halves[i]), tau_t[:, t : t + 1], bias[:, t : t + 1])
-
-        for t in range(PACK):
-            nc.scalar.activation(bias[:, t : t + 1], top[:, t : t + 1], ACT.Copy, scale=ntau[:, t : t + 1])
-            fetch_ea(t, 0)
-            if t not in HOLD:
-                fetch_ea(t, 1)
-
-        dk_raw = tile("dk_raw", [P, H], U32, tag="picked_words")
+        dk_raw = tile("dk_raw", [P, H], U32)
         dk = tile("dk", [P, H], U32)
         dks_raw = tile("dks_raw", [P, H], U8, tag="window")
         dks_dealt = tile("dks_dealt", [P, H], U8)
         nc.vector.tensor_copy(dks_raw[:], ds[:].indirect(k1_l[:]))
-        nc.vector.tensor_copy(dk_raw[:], dw[:].indirect(k1_l[:]))
+        for t in range(PACK):
+            leave_with_max(d[t], d_ps[t], 1.0, top[:, t : t + 1])
+        for t in range(PACK):
+            nc.scalar.activation(y[t][:], y_ps[t][:], ACT.Copy, scale=gs2[:, t : t + 1])
+            nc.scalar.activation(yg[:, t, halves[0]], y[t][:].indirect(entries(n2_l, halves[0])), ACT.Copy)
+        for t in range(PACK):
+            nc.gpsimd.tensor_tensor(bias[t][:], top[:, t : t + 1], ntau[:, t : t + 1], ALU.mult)
+            fetch_exp(ea[:, t, halves[0]], d[t], entries(n1_l, halves[0]), tau_t[:, t : t + 1], bias[t][:])
+        for t in range(PACK):
+            nc.scalar.activation(yg[:, t, halves[1]], y[t][:].indirect(entries(n2_l, halves[1])), ACT.Copy)
+        for c in pieces[1:]:
+            for t in range(PACK):
+                fetch_exp(ea[:, t, c], d[t], entries(n1_l, c), tau_t[:, t : t + 1], bias[t][:])
+
         deal(nc.vector.tensor_copy, dks_dealt[:], dks_raw[:])
+        nc.vector.tensor_copy(dk_raw[:], dw[:].indirect(k1_l[:]))
         deal(nc.vector.tensor_copy, dk[:], dk_raw[:])
         for q in range(4):
             nc.sync.dma_start(
@@ -199,37 +198,29 @@ def tile_picked_twqpxbesh_none_po_kernel(
         def interleave(engine_copy, dst, src):
             engine_copy(dst.rearrange("p (c i t) -> p c t i", i=4, t=PACK), src.rearrange("p t (c i) -> p c t i", i=4))
 
-        pieces = spans(PIECES)
+        z4 = {}
         for i, c in enumerate(pieces):
-            half = c.start // HALF
-            ch = slice(c.start - half * HALF, c.stop - half * HALF)
-            for t in range(PACK):
-                if i == 0:
-                    if t in ():
-                        nc.vector.tensor_scalar(y[t][:], y_ps[t][:], gs2[:, t : t + 1], None, op0=ALU.mult)
-                    else:
-                        nc.scalar.activation(y[t][:], y_ps[t][:], ACT.Copy, scale=gs2[:, t : t + 1])
-                if c.start == HALF and t in HOLD:
-                    fetch_ea(t, 1)
-                nc.scalar.activation(yg[:, t, c], y[t][:].indirect(entries(n2_l, c)), ACT.Copy)
-            for step in range(PACK + 2):
-                if step < PACK:
+            if c.start % HALF == 0:
+                ch = halves[c.start // HALF]
+                for t in range(PACK):
                     nc.vector.scalar_tensor_tensor(
-                        diff[:, step, c], y_ps[step][:, c], gs2[:, step : step + 1], yg[:, step, c],
-                        op0=ALU.mult, op1=ALU.subtract,
+                        diff[:, t, ch], y_ps[t][:, ch], gs2[:, t : t + 1], yg[:, t, ch], op0=ALU.mult, op1=ALU.subtract
                     )
+            for step in range(PACK + 1):
+                if step < PACK:
+                    t = step
+                    eng = nc.gpsimd if False else nc.vector
+                    eng.tensor_tensor(gated[:, t, c], diff[:, t, c], ea[:, t, c], ALU.mult)
                 if 0 <= step - 1 < PACK:
                     t = step - 1
-                    eng = nc.gpsimd if False else nc.vector
-                    eng.tensor_tensor(gated[:, t, c], diff[:, t, c], ea[t][half][:, ch], ALU.mult)
-                if 0 <= step - 2 < PACK:
-                    t = step - 2
                     nc.vector.scalar_tensor_tensor(
                         zb[:, t, c], d_ps[t][:, c], gsh[:, t : t + 1], gated[:, t, c], op0=ALU.mult, op1=ALU.add
                     )
-            z4 = tile(f"z4_{i}", [P, PIECES[i] * PACK], BF16)
-            interleave(nc.scalar.copy if i in () else nc.vector.tensor_copy, z4[:], zb[:, :, c])
-            nc.vector.quantize_mx(z_codes[:, c].bitcast(FP8X4), z_scales[:, c], z4[:])
+            z4[i] = tile(f"z4_{i}", [P, PIECES[i] * PACK], BF16)
+            if i > 0:
+                nc.vector.quantize_mx(z_codes[:, pieces[i - 1]].bitcast(FP8X4), z_scales[:, pieces[i - 1]], z4[i - 1][:])
+            interleave(nc.scalar.copy if i in (0,) else nc.vector.tensor_copy, z4[i][:], zb[:, :, c])
+        nc.vector.quantize_mx(z_codes[:, c].bitcast(FP8X4), z_scales[:, c], z4[i][:])
         h_ps = [ps.tile([P, S], F32, name=f"h_ps{t}", tag=f"b{t}") for t in range(PACK)]
         for c in pieces:
             for t in range(PACK):
@@ -288,7 +279,9 @@ def tile_picked_twqpxbesh_none_po_kernel(
             if 0 <= step - 2 < len(chunks):
                 c = chunks[step - 2]
                 nc.vector.quantize_mx(o_codes[:, c].bitcast(FP8X4), o_scales[:, c], o4[step - 2][:])
-                nc.sync.dma_start(out_words[:, c], o_codes[:, c].bitcast(I32))
+                if step % 2:
+                    pair = slice(c.stop - HALF, c.stop)
+                    nc.sync.dma_start(out_words[:, pair], o_codes[:, pair].bitcast(I32))
         for q in range(4):
             queue = nc.scalar if q % 2 else nc.sync
             queue.dma_start(out_2[0, 4 * q : 4 * q + 4, :].bitcast(I32), o_scales[32 * q : 32 * q + 4, :].bitcast(I32))

@@ -55,8 +55,10 @@ def tile_picked_twqpxbesh_none_po_kernel(
             queue.dma_start(dst[:], src.rearrange("(p t) o -> p (t o)", t=PACK))
             return dst
 
-        def deal(engine_copy, dst, src):
-            engine_copy(dst.rearrange("p (t m) -> p t m", t=PACK), src.rearrange("p (m t) -> p t m", t=PACK))
+        def deal(engine_copy, dst, src, run):
+            engine_copy(
+                dst.rearrange("p (t m i) -> p m t i", t=PACK, i=run), src.rearrange("p (m i t) -> p m t i", t=PACK, i=run)
+            )
 
         def entries(lst, c):
             return lst[:, c.start // 16 : c.stop // 16]
@@ -68,7 +70,7 @@ def tile_picked_twqpxbesh_none_po_kernel(
         dk_scales = tile("dk_scales", [P, H], U8)
         zero(nc.gpsimd, xs)
         zero(nc.gpsimd, w1s_raw)
-        zero(nc.vector, w2s_raw)
+        zero(nc.gpsimd, w2s_raw)
         zero(nc.vector, ds)
         zero(nc.vector, dk_scales)
 
@@ -87,13 +89,13 @@ def tile_picked_twqpxbesh_none_po_kernel(
         load_scale_rows(nc.sync, w1s_raw, w1_scales, 1)
         load_scale_rows(nc.sync, w1s_raw, w1_scales, 2)
         load_scale_rows(nc.sync, w1s_raw, w1_scales, 3)
-        two_l = load_list("two_l", two)
-        nc.sync.dma_start(w2w_raw[:].bitcast(I32), w2_words[0].bitcast(I32))
-        gs_t = load_rows(nc.sync, "gs_t", gs)
         load_scale_rows(nc.sync, w2s_raw, w2_scales, 0)
         load_scale_rows(nc.sync, w2s_raw, w2_scales, 1)
         load_scale_rows(nc.sync, w2s_raw, w2_scales, 2)
         load_scale_rows(nc.sync, w2s_raw, w2_scales, 3)
+        two_l = load_list("two_l", two)
+        gs_t = load_rows(nc.sync, "gs_t", gs)
+        nc.sync.dma_start(w2w_raw[:].bitcast(I32), w2_words[0].bitcast(I32))
         k1_l = load_list("k1_l", k1)
         nc.sync.dma_start(ds[0:P:8, :].bitcast(I32), d_scales[0].bitcast(I32))
         tau_t = load_rows(nc.sync, "tau_t", tau)
@@ -111,12 +113,11 @@ def tile_picked_twqpxbesh_none_po_kernel(
         gsh = tile("gsh", [P, PACK], F32)
         ntau = tile("ntau", [P, PACK], F32)
         ntau2 = tile("ntau2", [P, PACK], F32)
-        deal(nc.scalar.copy, w1w[:].bitcast(U16), w1w_raw[:].bitcast(U16))
+        deal(nc.scalar.copy, w1w[:].bitcast(U16), w1w_raw[:].bitcast(U16), 8)
         nc.scalar.activation(gs2[:], gs_t[:], ACT.Copy, scale=2.0)
-        deal(nc.scalar.copy, w2w[:].bitcast(U16), w2w_raw[:].bitcast(U16))
-        deal(nc.gpsimd.tensor_copy, w2s[:], w2s_raw[:])
+        deal(nc.scalar.copy, w2w[:].bitcast(U16), w2w_raw[:].bitcast(U16), 8)
         nc.gpsimd.tensor_scalar(gsh[:], gs_t[:], -0.5, 0.0, op0=ALU.mult, op1=ALU.add)
-        nc.gpsimd.tensor_scalar(ntau[:], tau_t[:], -1.0, 0.0, op0=ALU.mult, op1=ALU.add)
+        nc.scalar.activation(ntau[:], tau_t[:], ACT.Copy, scale=-1.0)
         nc.gpsimd.tensor_scalar(ntau2[:], tau2_t[:], -1.0, 0.0, op0=ALU.mult, op1=ALU.add)
 
         x1s = tile("x1s", [P, S], U8)
@@ -125,7 +126,8 @@ def tile_picked_twqpxbesh_none_po_kernel(
         x2w = tile("x2w", [P, S], U32)
         nc.vector.tensor_copy(x1s[:], xs[:].indirect(offs_l[:]))
         nc.vector.tensor_copy(x1w[:], xw[:].indirect(offs_l[:]))
-        deal(nc.vector.tensor_copy, w1s[:], w1s_raw[:])
+        deal(nc.vector.tensor_copy, w1s[:], w1s_raw[:], 16)
+        deal(nc.vector.tensor_copy, w2s[:], w2s_raw[:], 16)
         nc.vector.tensor_copy(x2s[:], xs[:].indirect(two_l[:]))
         nc.vector.tensor_copy(x2w[:], xw[:].indirect(two_l[:]))
 
@@ -173,7 +175,7 @@ def tile_picked_twqpxbesh_none_po_kernel(
             nc.scalar.activation(y[t][:], y_ps[t][:], ACT.Copy, scale=gs2[:, t : t + 1])
             nc.scalar.activation(yg[:, t, halves[0]], y[t][:].indirect(entries(n2_l, halves[0])), ACT.Copy)
         for t in range(PACK):
-            nc.gpsimd.tensor_tensor(bias[t][:], top[:, t : t + 1], ntau[:, t : t + 1], ALU.mult)
+            nc.scalar.activation(bias[t][:], top[:, t : t + 1], ACT.Copy, scale=ntau[:, t : t + 1])
             fetch_exp(ea[:, t, halves[0]], d[t], entries(n1_l, halves[0]), tau_t[:, t : t + 1], bias[t][:])
         for t in range(PACK):
             nc.scalar.activation(yg[:, t, halves[1]], y[t][:].indirect(entries(n2_l, halves[1])), ACT.Copy)
@@ -181,9 +183,9 @@ def tile_picked_twqpxbesh_none_po_kernel(
             for t in range(PACK):
                 fetch_exp(ea[:, t, c], d[t], entries(n1_l, c), tau_t[:, t : t + 1], bias[t][:])
 
-        deal(nc.vector.tensor_copy, dks_dealt[:], dks_raw[:])
+        deal(nc.vector.tensor_copy, dks_dealt[:], dks_raw[:], 16)
         nc.vector.tensor_copy(dk_raw[:], dw[:].indirect(k1_l[:]))
-        deal(nc.vector.tensor_copy, dk[:], dk_raw[:])
+        deal(nc.vector.tensor_copy, dk[:], dk_raw[:], 4)
         for q in range(4):
             nc.sync.dma_start(
                 dk_scales[32 * q : 32 * q + 4, :].bitcast(I32), dks_dealt[32 * q : 32 * q + 32 : 8, :].bitcast(I32)

@@ -89,14 +89,14 @@ def tile_picked_twqpxbesh_none_po_kernel(
         load_scale_rows(nc.sync, w1s_raw, w1_scales, 1)
         load_scale_rows(nc.sync, w1s_raw, w1_scales, 2)
         load_scale_rows(nc.sync, w1s_raw, w1_scales, 3)
+        two_l = load_list("two_l", two)
+        nc.sync.dma_start(w2w_raw[:].bitcast(I32), w2_words[0].bitcast(I32))
+        gs_t = load_rows(nc.sync, "gs_t", gs)
+        k1_l = load_list("k1_l", k1)
         load_scale_rows(nc.sync, w2s_raw, w2_scales, 0)
         load_scale_rows(nc.sync, w2s_raw, w2_scales, 1)
         load_scale_rows(nc.sync, w2s_raw, w2_scales, 2)
         load_scale_rows(nc.sync, w2s_raw, w2_scales, 3)
-        two_l = load_list("two_l", two)
-        gs_t = load_rows(nc.sync, "gs_t", gs)
-        nc.sync.dma_start(w2w_raw[:].bitcast(I32), w2_words[0].bitcast(I32))
-        k1_l = load_list("k1_l", k1)
         nc.sync.dma_start(ds[0:P:8, :].bitcast(I32), d_scales[0].bitcast(I32))
         tau_t = load_rows(nc.sync, "tau_t", tau)
         n2_l = load_list("n2_l", n2)
@@ -117,7 +117,7 @@ def tile_picked_twqpxbesh_none_po_kernel(
         nc.scalar.activation(gs2[:], gs_t[:], ACT.Copy, scale=2.0)
         deal(nc.scalar.copy, w2w[:].bitcast(U16), w2w_raw[:].bitcast(U16), 8)
         nc.gpsimd.tensor_scalar(gsh[:], gs_t[:], -0.5, 0.0, op0=ALU.mult, op1=ALU.add)
-        nc.scalar.activation(ntau[:], tau_t[:], ACT.Copy, scale=-1.0)
+        nc.gpsimd.tensor_scalar(ntau[:], tau_t[:], -1.0, 0.0, op0=ALU.mult, op1=ALU.add)
         nc.gpsimd.tensor_scalar(ntau2[:], tau2_t[:], -1.0, 0.0, op0=ALU.mult, op1=ALU.add)
 
         x1s = tile("x1s", [P, S], U8)
@@ -175,10 +175,11 @@ def tile_picked_twqpxbesh_none_po_kernel(
             nc.scalar.activation(y[t][:], y_ps[t][:], ACT.Copy, scale=gs2[:, t : t + 1])
             nc.scalar.activation(yg[:, t, halves[0]], y[t][:].indirect(entries(n2_l, halves[0])), ACT.Copy)
         for t in range(PACK):
-            nc.scalar.activation(bias[t][:], top[:, t : t + 1], ACT.Copy, scale=ntau[:, t : t + 1])
+            nc.gpsimd.tensor_tensor(bias[t][:], top[:, t : t + 1], ntau[:, t : t + 1], ALU.mult)
             fetch_exp(ea[:, t, halves[0]], d[t], entries(n1_l, halves[0]), tau_t[:, t : t + 1], bias[t][:])
         for t in range(PACK):
-            nc.scalar.activation(yg[:, t, halves[1]], y[t][:].indirect(entries(n2_l, halves[1])), ACT.Copy)
+            if t not in ():
+                nc.scalar.activation(yg[:, t, halves[1]], y[t][:].indirect(entries(n2_l, halves[1])), ACT.Copy)
         for c in pieces[1:]:
             for t in range(PACK):
                 fetch_exp(ea[:, t, c], d[t], entries(n1_l, c), tau_t[:, t : t + 1], bias[t][:])
@@ -191,6 +192,7 @@ def tile_picked_twqpxbesh_none_po_kernel(
                 dk_scales[32 * q : 32 * q + 4, :].bitcast(I32), dks_dealt[32 * q : 32 * q + 32 : 8, :].bitcast(I32)
             )
 
+        ygv = None
         diff = tile("diff", [P, PACK, S], F32)
         gated = tile("gated", [P, PACK, S], F32)
         zb = tile("zb", [P, PACK, S], BF16)
@@ -204,14 +206,16 @@ def tile_picked_twqpxbesh_none_po_kernel(
         for i, c in enumerate(pieces):
             if c.start % HALF == 0:
                 ch = halves[c.start // HALF]
+                for t in () if c.start == HALF else ():
+                    nc.vector.tensor_copy(ygv[:, t, :], y[t][:].indirect(entries(n2_l, halves[1])))
                 for t in range(PACK):
                     nc.vector.scalar_tensor_tensor(
-                        diff[:, t, ch], y_ps[t][:, ch], gs2[:, t : t + 1], yg[:, t, ch], op0=ALU.mult, op1=ALU.subtract
+                        diff[:, t, ch], y_ps[t][:, ch], gs2[:, t : t + 1], ygv[:, t, :] if c.start == HALF and t in () else yg[:, t, ch], op0=ALU.mult, op1=ALU.subtract
                     )
             for step in range(PACK + 1):
                 if step < PACK:
                     t = step
-                    eng = nc.gpsimd if False else nc.vector
+                    eng = nc.gpsimd if i == 0 else nc.vector
                     eng.tensor_tensor(gated[:, t, c], diff[:, t, c], ea[:, t, c], ALU.mult)
                 if 0 <= step - 1 < PACK:
                     t = step - 1
@@ -249,15 +253,15 @@ def tile_picked_twqpxbesh_none_po_kernel(
             if t == 0:
                 nc.scalar.activation(bias2[t][:], top2[:, t : t + 1], ACT.Copy, scale=ntau2[:, t : t + 1])
             else:
-                nc.vector.tensor_tensor(bias2[t][:], top2[:, t : t + 1], ntau2[:, t : t + 1], ALU.mult)
+                nc.gpsimd.tensor_tensor(bias2[t][:], top2[:, t : t + 1], ntau2[:, t : t + 1], ALU.mult)
         for t in range(PACK):
             nc.scalar.activation(own[:, t, :], h[t][:], ACT.Exp, bias=bias2[t][:], scale=tau2_t[:, t : t + 1])
             for c in halves:
                 fetch_exp(ea2[:, t, c], h[t], entries(n3_l, c), tau2_t[:, t : t + 1], bias2[t][:])
             nc.vector.scalar_tensor_tensor(num[:, t, :], h_ps[t][:], 0.125, own[:, t, :], op0=ALU.mult, op1=ALU.mult)
-            for c in halves:
+            for c in halves if t == PACK - 1 else spans((S,)):
                 nc.vector.scalar_tensor_tensor(den[:, t, c], own[:, t, c], 0.25, ea2[:, t, c], op0=ALU.add, op1=ALU.add)
-            for c in halves:
+            for c in halves if t == PACK - 1 else spans((S,)):
                 nc.vector.tensor_tensor(den_sq[:, t, c], den[:, t, c], den[:, t, c], ALU.mult)
 
         inv = tile("inv", [P, PACK, S], F32)

from contextlib import ExitStack

import concourse.mybir as mybir

K, T, S, H, G = 512, 1024, 512, 512, 2048
FLOPS = 3 * 2 * K * H * S

F32 = mybir.dt.float32
BF16 = mybir.dt.bfloat16
I32 = mybir.dt.int32
U32 = mybir.dt.uint32
U16 = mybir.dt.uint16
U8 = mybir.dt.uint8
FP8X4 = mybir.dt.float8_e4m3fn_x4
FP4X4 = mybir.dt.float4_e2m1fn_x4
ALU = mybir.AluOpType
ACT = mybir.ActivationFunctionType

P = 128
PACK = 4
HALF = S // 2
PIECES = (256, 256)
CHUNKS = (128, 128, 128, 128)


def spans(widths):
    return [slice(sum(widths[:i]), sum(widths[: i + 1])) for i in range(len(widths))]


def tile_picked_twqpxbesh_none_po_kernel(
    tc, x_words, x_scales, w1_words, w1_scales, w2_words, w2_scales, tau, gs, d_words, d_scales, tau2,
    offs, two, n1, n2, k1, n3, out_0, out_1, out_2,
):
    nc = tc.nc
    with ExitStack() as ctx:
        sb = ctx.enter_context(tc.tile_pool(name="sb", bufs=1))
        ps = ctx.enter_context(tc.psum_pool(name="ps", bufs=1))

        def tile(name, shape, dtype, tag=""):
            return sb.tile(shape, dtype, name=name, tag=tag or name, align_bytes=64)

        def load_list(name, src):
            dst = sb.tile([P, S // 16], U16, name=name)
            nc.sync.dma_start(dst[:], src)
            return dst

        def zero(engine, dst):
            engine.memset(dst[:].bitcast(I32), 0)

        def load_scale_rows(queue, dst, src, q):
            queue.dma_start(dst[32 * q : 32 * q + 4, :].bitcast(I32), src[0, 4 * q : 4 * q + 4, :].bitcast(I32))

        def load_rows(queue, name, src):
            dst = tile(name, [P, PACK], F32)
            queue.dma_start(dst[:], src.rearrange("(p t) o -> p (t o)", t=PACK))
            return dst

        def deal(engine_copy, dst, src, run):
            engine_copy(
                dst.rearrange("p (t m i) -> p m t i", t=PACK, i=run), src.rearrange("p (m i t) -> p m t i", t=PACK, i=run)
            )

        def entries(lst, c):
            return lst[:, c.start // 16 : c.stop // 16]

        xs = tile("xs", [P, T], U8)
        w2s_raw = tile("w2s_raw", [P, H], U8)
        w1s_raw = tile("w1s_raw", [P, H], U8)
        ds = tile("ds", [P, G], U8)
        dk_scales = tile("dk_scales", [P, H], U8)
        zero(nc.gpsimd, xs)
        zero(nc.gpsimd, w1s_raw)
        zero(nc.gpsimd, w2s_raw)
        zero(nc.vector, ds)
        zero(nc.vector, dk_scales)

        xw = tile("xw", [P, T], U32, tag="window")
        w2w_raw = tile("w2w_raw", [P, 2 * H], U8)
        w1w_raw = tile("w1w_raw", [P, 2 * H], U8)
        dw = tile("dw", [P, G], U32)
        offs_l = load_list("offs_l", offs)
        load_scale_rows(nc.sync, xs, x_scales, 0)
        load_scale_rows(nc.scalar, xs, x_scales, 1)
        load_scale_rows(nc.scalar, xs, x_scales, 2)
        load_scale_rows(nc.scalar, xs, x_scales, 3)
        nc.sync.dma_start(w1w_raw[:].bitcast(I32), w1_words[0].bitcast(I32))
        load_scale_rows(nc.sync, w1s_raw, w1_scales, 0)
        nc.sync.dma_start(xw[:].bitcast(I32), x_words[0].rearrange("p n t -> p (n t)").bitcast(I32))
        load_scale_rows(nc.sync, w1s_raw, w1_scales, 1)
        load_scale_rows(nc.sync, w1s_raw, w1_scales, 2)
        load_scale_rows(nc.sync, w1s_raw, w1_scales, 3)
        two_l = load_list("two_l", two)
        nc.sync.dma_start(w2w_raw[:].bitcast(I32), w2_words[0].bitcast(I32))
        gs_t = load_rows(nc.sync, "gs_t", gs)
        k1_l = load_list("k1_l", k1)
        load_scale_rows(nc.sync, w2s_raw, w2_scales, 0)
        load_scale_rows(nc.sync, w2s_raw, w2_scales, 1)
        load_scale_rows(nc.sync, w2s_raw, w2_scales, 2)
        load_scale_rows(nc.sync, w2s_raw, w2_scales, 3)
        nc.sync.dma_start(ds[0:P:8, :].bitcast(I32), d_scales[0].bitcast(I32))
        tau_t = load_rows(nc.sync, "tau_t", tau)
        n2_l = load_list("n2_l", n2)
        n1_l = load_list("n1_l", n1)
        nc.sync.dma_start(dw[:].bitcast(I32), d_words[0].rearrange("p n t -> p (n t)").bitcast(I32))
        tau2_t = load_rows(nc.sync, "tau2_t", tau2)
        n3_l = load_list("n3_l", n3)

        w2w = tile("w2w", [P, 2 * H], U8)
        w2s = tile("w2s", [P, H], U8)
        w1w = tile("w1w", [P, 2 * H], U8)
        w1s = tile("w1s", [P, H], U8)
        gs2 = tile("gs2", [P, PACK], F32)
        gsh = tile("gsh", [P, PACK], F32)
        ntau = tile("ntau", [P, PACK], F32)
        ntau2 = tile("ntau2", [P, PACK], F32)
        deal(nc.scalar.copy, w1w[:].bitcast(U16), w1w_raw[:].bitcast(U16), 8)
        nc.scalar.activation(gs2[:], gs_t[:], ACT.Copy, scale=2.0)
        deal(nc.scalar.copy, w2w[:].bitcast(U16), w2w_raw[:].bitcast(U16), 8)
        nc.gpsimd.tensor_scalar(gsh[:], gs_t[:], -0.5, 0.0, op0=ALU.mult, op1=ALU.add)
        nc.gpsimd.tensor_scalar(ntau[:], tau_t[:], -1.0, 0.0, op0=ALU.mult, op1=ALU.add)
        nc.gpsimd.tensor_scalar(ntau2[:], tau2_t[:], -1.0, 0.0, op0=ALU.mult, op1=ALU.add)

        x1s = tile("x1s", [P, S], U8)
        x1w = tile("x1w", [P, S], U32)
        x2s = tile("x2s", [P, S], U8)
        x2w = tile("x2w", [P, S], U32)
        nc.vector.tensor_copy(x1s[:], xs[:].indirect(offs_l[:]))
        nc.vector.tensor_copy(x1w[:], xw[:].indirect(offs_l[:]))
        deal(nc.vector.tensor_copy, w1s[:], w1s_raw[:], 16)
        deal(nc.vector.tensor_copy, w2s[:], w2s_raw[:], 16)
        nc.vector.tensor_copy(x2s[:], xs[:].indirect(two_l[:]))
        nc.vector.tensor_copy(x2w[:], xw[:].indirect(two_l[:]))

        def project(bank, words, scales, xwords, xscales, t):
            nc.tensor.matmul_mx(
                bank[:],
                lhsT=words[:, 2 * P * t : 2 * P * (t + 1)].bitcast(FP4X4),
                lhsT_scale=scales[:, P * t : P * (t + 1)],
                rhs=xwords[:].bitcast(FP8X4),
                rhs_scale=xscales[:],
                start=True,
                stop=True,
            )

        d_ps = [ps.tile([P, S], F32, name=f"d_ps{t}", tag=f"a{t}") for t in range(PACK)]
        y_ps = [ps.tile([P, S], F32, name=f"y_ps{t}", tag=f"b{t}") for t in range(PACK)]
        for t in range(PACK):
            project(y_ps[t], w1w, w1s, x1w, x1s, t)
        for t in range(PACK):
            project(d_ps[t], w2w, w2s, x2w, x2s, t)

        d = [tile(f"d{t}", [P, S], F32) for t in range(PACK)]
        y = [tile(f"y{t}", [P, S], F32) for t in range(PACK)]
        top = tile("top", [P, PACK], F32)
        bias = [tile(f"bias_{t}", [P, 1], F32) for t in range(PACK)]
        yg = tile("yg", [P, PACK, S], F32)
        ea = tile("ea", [P, PACK, S], F32)
        halves = spans((HALF, HALF))
        pieces = spans(PIECES)

        def leave_with_max(dst, bank, factor, largest):
            nc.vector.tensor_scalar(dst[:], bank[:], factor, None, op0=ALU.mult, op1=ALU.max, accum_out=largest)

        def fetch_exp(dst, window, offsets, scale, shift):
            nc.scalar.activation(dst, window[:].indirect(offsets), ACT.Exp, bias=shift, scale=scale)

        dk_raw = tile("dk_raw", [P, H], U32)
        dk = tile("dk", [P, H], U32)
        dks_raw = tile("dks_raw", [P, H], U8, tag="window")
        dks_dealt = tile("dks_dealt", [P, H], U8)
        nc.vector.tensor_copy(dks_raw[:], ds[:].indirect(k1_l[:]))
        for t in range(PACK):
            leave_with_max(d[t], d_ps[t], 1.0, top[:, t : t + 1])
        for t in range(PACK):
            nc.scalar.activation(y[t][:], y_ps[t][:], ACT.Copy, scale=gs2[:, t : t + 1])
            nc.scalar.activation(yg[:, t, halves[0]], y[t][:].indirect(entries(n2_l, halves[0])), ACT.Copy)
        for t in range(PACK):
            nc.gpsimd.tensor_tensor(bias[t][:], top[:, t : t + 1], ntau[:, t : t + 1], ALU.mult)
            fetch_exp(ea[:, t, halves[0]], d[t], entries(n1_l, halves[0]), tau_t[:, t : t + 1], bias[t][:])
        for t in range(PACK):
            if t not in ():
                nc.scalar.activation(yg[:, t, halves[1]], y[t][:].indirect(entries(n2_l, halves[1])), ACT.Copy)
        for c in pieces[1:]:
            for t in range(PACK):
                fetch_exp(ea[:, t, c], d[t], entries(n1_l, c), tau_t[:, t : t + 1], bias[t][:])

        deal(nc.vector.tensor_copy, dks_dealt[:], dks_raw[:], 16)
        nc.vector.tensor_copy(dk_raw[:], dw[:].indirect(k1_l[:]))
        deal(nc.vector.tensor_copy, dk[:], dk_raw[:], 4)
        for q in range(4):
            nc.sync.dma_start(
                dk_scales[32 * q : 32 * q + 4, :].bitcast(I32), dks_dealt[32 * q : 32 * q + 32 : 8, :].bitcast(I32)
            )

        ygv = None
        diff = tile("diff", [P, PACK, S], F32)
        gated = tile("gated", [P, PACK, S], F32)
        zb = tile("zb", [P, PACK, S], BF16)
        z_codes = tile("z_codes", [P, S], U32)
        z_scales = tile("z_scales", [P, S], U8)

        def interleave(engine_copy, dst, src):
            engine_copy(dst.rearrange("p (c i t) -> p c t i", i=4, t=PACK), src.rearrange("p t (c i) -> p c t i", i=4))

        z4 = {}
        for i, c in enumerate(pieces):
            if c.start % HALF == 0:
                ch = halves[c.start // HALF]
                for t in () if c.start == HALF else ():
                    nc.vector.tensor_copy(ygv[:, t, :], y[t][:].indirect(entries(n2_l, halves[1])))
                for t in range(PACK):
                    nc.vector.scalar_tensor_tensor(
                        diff[:, t, ch], y_ps[t][:, ch], gs2[:, t : t + 1], ygv[:, t, :] if c.start == HALF and t in () else yg[:, t, ch], op0=ALU.mult, op1=ALU.subtract
                    )
            for step in range(PACK + 1):
                if step < PACK:
                    t = step
                    eng = nc.gpsimd if i == 0 else nc.vector
                    eng.tensor_tensor(gated[:, t, c], diff[:, t, c], ea[:, t, c], ALU.mult)
                if 0 <= step - 1 < PACK:
                    t = step - 1
                    nc.vector.scalar_tensor_tensor(
                        zb[:, t, c], d_ps[t][:, c], gsh[:, t : t + 1], gated[:, t, c], op0=ALU.mult, op1=ALU.add
                    )
            z4[i] = tile(f"z4_{i}", [P, PIECES[i] * PACK], BF16)
            if i > 0:
                nc.vector.quantize_mx(z_codes[:, pieces[i - 1]].bitcast(FP8X4), z_scales[:, pieces[i - 1]], z4[i - 1][:])
            interleave(nc.scalar.copy if i in (0,) else nc.vector.tensor_copy, z4[i][:], zb[:, :, c])
        nc.vector.quantize_mx(z_codes[:, c].bitcast(FP8X4), z_scales[:, c], z4[i][:])
        h_ps = [ps.tile([P, S], F32, name=f"h_ps{t}", tag=f"b{t}") for t in range(PACK)]
        for c in pieces:
            for t in range(PACK):
                nc.tensor.matmul_mx(
                    h_ps[t][:, c],
                    lhsT=dk[:, P * t : P * (t + 1)].bitcast(FP8X4),
                    lhsT_scale=dk_scales[:, P * t : P * (t + 1)],
                    rhs=z_codes[:, c].bitcast(FP8X4),
                    rhs_scale=z_scales[:, c],
                    start=True,
                    stop=True,
                )

        h = [tile(f"h{t}", [P, S], F32) for t in range(PACK)]
        top2 = tile("top2", [P, PACK], F32)
        bias2 = [tile(f"bias2_{t}", [P, 1], F32) for t in range(PACK)]
        own = tile("own", [P, PACK, S], F32)
        ea2 = tile("ea2", [P, PACK, S], F32)
        den = tile("den", [P, PACK, S], F32)
        num = tile("num", [P, PACK, S], F32)
        den_sq = tile("den_sq", [P, PACK, S], F32)
        for t in range(PACK):
            leave_with_max(h[t], h_ps[t], 0.0625, top2[:, t : t + 1])
            if t == 0:
                nc.scalar.activation(bias2[t][:], top2[:, t : t + 1], ACT.Copy, scale=ntau2[:, t : t + 1])
            else:
                nc.gpsimd.tensor_tensor(bias2[t][:], top2[:, t : t + 1], ntau2[:, t : t + 1], ALU.mult)
        for t in range(PACK):
            nc.scalar.activation(own[:, t, :], h[t][:], ACT.Exp, bias=bias2[t][:], scale=tau2_t[:, t : t + 1])
            for c in halves:
                fetch_exp(ea2[:, t, c], h[t], entries(n3_l, c), tau2_t[:, t : t + 1], bias2[t][:])
            nc.vector.scalar_tensor_tensor(num[:, t, :], h_ps[t][:], 0.125, own[:, t, :], op0=ALU.mult, op1=ALU.mult)
            for c in halves if t == PACK - 1 else spans((S,)):
                nc.vector.scalar_tensor_tensor(den[:, t, c], own[:, t, c], 0.25, ea2[:, t, c], op0=ALU.add, op1=ALU.add)
            for c in halves if t == PACK - 1 else spans((S,)):
                nc.vector.tensor_tensor(den_sq[:, t, c], den[:, t, c], den[:, t, c], ALU.mult)

        inv = tile("inv", [P, PACK, S], F32)
        res = tile("res", [P, PACK, S], F32)
        o_codes = tile("o_codes", [P, S], U32)
        o_scales = tile("o_scales", [P, S], U8)
        out_rows = out_0.rearrange("(p t) c -> p t c", t=PACK)
        out_words = out_1[0].rearrange("p n t -> p (n t)").bitcast(I32)
        chunks = spans(CHUNKS)
        o4 = [tile(f"o4_{i}", [P, CHUNKS[i] * PACK], BF16) for i in range(len(chunks))]
        for c in chunks:
            nc.scalar.activation(inv[:, :, c], den_sq[:, :, c], ACT.Abs_reciprocal_sqrt)
        for step in range(len(chunks) + 2):
            if step < len(chunks):
                c = chunks[step]
                nc.vector.tensor_tensor(res[:, :, c], num[:, :, c], inv[:, :, c], ALU.mult)
                nc.sync.dma_start(out_rows[:, :, c], res[:, :, c])
            if 0 <= step - 1 < len(chunks):
                copy = nc.scalar.copy if step - 1 in (0, 1) else nc.vector.tensor_copy
                interleave(copy, o4[step - 1][:], res[:, :, chunks[step - 1]])
            if 0 <= step - 2 < len(chunks):
                c = chunks[step - 2]
                nc.vector.quantize_mx(o_codes[:, c].bitcast(FP8X4), o_scales[:, c], o4[step - 2][:])
                if step % 2:
                    pair = slice(c.stop - HALF, c.stop)
                    nc.sync.dma_start(out_words[:, pair], o_codes[:, pair].bitcast(I32))
        for q in range(4):
            queue = nc.scalar if q % 2 else nc.sync
            queue.dma_start(out_2[0, 4 * q : 4 * q + 4, :].bitcast(I32), o_scales[32 * q : 32 * q + 4, :].bitcast(I32))
